import numpy as np
import ml_dtypes


def mxq(x, axis, fmt="e4m3"):
    dtype, down = {"e4m3": (ml_dtypes.float8_e4m3fn, 7), "e5m2": (ml_dtypes.float8_e5m2, 14)}[fmt]
    v = np.moveaxis(np.asarray(x, np.float32).astype(ml_dtypes.bfloat16).astype(np.float64), axis, -1)
    blocks = v.reshape(v.shape[:-1] + (-1, 32))
    amax = np.abs(blocks).max(-1, keepdims=True)
    byte = np.maximum(np.where(amax > 0, np.frexp(amax)[1] - 1 + 127, 0) - down, 1)
    scale = np.exp2(byte - 127.0)
    codes = (blocks / scale).astype(np.float32).astype(dtype).astype(np.float64)
    return np.moveaxis((codes * scale).reshape(v.shape), -1, axis)


WIDE = False


def mx_kscale(k):
    if not WIDE:
        return np.ones(k)
    levels = np.array([10, -10, 5, -5, 0])
    if k % 512:
        return np.exp2(np.random.permutation(np.resize(levels, k // 32))).repeat(32)
    a = np.empty((k // 512, 16))
    for p in range(k // 512):
        a[p, :8] = np.random.permutation(np.resize(levels, 8))
        for g in range(8):
            far = levels[np.abs(levels - a[p, g]) >= 10]
            a[p, g + 8] = far[np.random.randint(len(far))]
    return np.exp2(a.ravel()).repeat(32)


def f64(x):
    return np.asarray(x).astype(np.float64)


def striped(idx):
    return np.tile(idx.reshape(-1, 16).T, (8, 1)).astype(np.uint16)


def unstriped(offs):
    return offs[:16].T.reshape(-1).astype(np.int64)


E2M1 = np.array([0.0, 0.5, 1.0, 1.5, 2.0, 3.0, 4.0, 6.0, -0.0, -0.5, -1.0, -1.5, -2.0, -3.0, -4.0, -6.0])


def pack_weight(w, fmt):
    k, n = w.shape
    w = f64(np.asarray(w, np.float32).astype(ml_dtypes.bfloat16)).reshape(k // 32, 32, n)
    amax = np.abs(w).max(1)
    if fmt == "e4m3":
        byte = np.frexp(amax)[1] - 1 + 127 - 7
    else:
        mant, ex = np.frexp(amax / 6.0)
        byte = np.where(mant > 0.5, ex, ex - 1) + 127
    byte = np.clip(np.where(amax > 0, byte, 1), 1, 254)
    scaled = (w * np.exp2(127.0 - byte)[:, None, :]).reshape(k, n).astype(np.float32)
    by_word = np.ascontiguousarray(scaled.reshape(k // 512, 128, 4, n).transpose(0, 1, 3, 2))
    if fmt == "e4m3":
        words = by_word.astype(ml_dtypes.float8_e4m3fn).view(np.uint8)
    else:
        c = by_word.astype(ml_dtypes.float4_e2m1fn).view(np.uint8) & 0xF
        words = (c[..., 0::2] | (c[..., 1::2] << 4)).reshape(k // 512, 128, 2 * n)
    return np.ascontiguousarray(words), np.ascontiguousarray(byte.astype(np.uint8).reshape(k // 512, 16, n))


def unpack_weight(words, scales, fmt):
    g, _, n = scales.shape
    words = np.ascontiguousarray(words).reshape(g, 128, n, -1)
    if fmt == "e4m3":
        vals = words.view(ml_dtypes.float8_e4m3fn).astype(np.float64)
    else:
        nib = np.empty((g, 128, n, 4), np.uint8)
        nib[..., 0::2] = words & 0xF
        nib[..., 1::2] = words >> 4
        vals = E2M1[nib]
    vals = vals * np.repeat(np.exp2(scales.astype(np.float64) - 127.0), 8, axis=1)[..., None]
    return vals.transpose(0, 1, 3, 2).reshape(g * 512, n)


def gelu(v):
    return 0.5 * v * (1.0 + np.tanh(np.sqrt(2.0 / np.pi) * (v + 0.044715 * v**3)))


def bf(x):
    return np.asarray(x, np.float32).astype(ml_dtypes.bfloat16)


def planes(Y):
    n, m = Y.shape
    b = f64(bf(Y)).reshape(n // 32, 32, m)
    amax = np.abs(b).max(1)
    byte = np.clip(np.where(amax > 0, np.frexp(amax)[1] - 1 + 127 - 7, 1), 1, 254)
    codes = (b * np.exp2(127.0 - byte)[:, None, :]).reshape(n, m).astype(np.float32).astype(ml_dtypes.float8_e4m3fn).view(np.uint8)
    words = codes.reshape(n // 512, 128, 4, m).transpose(0, 1, 3, 2)
    return np.ascontiguousarray(words), np.ascontiguousarray(byte.astype(np.uint8).reshape(n // 512, 16, m))


T, S, TG, P, K, M, H, N = 4096, 1024, 2048, 512, 1024, 1536, 1024, 512

def setup_inputs():
    n = np.random.standard_normal
    s = mx_kscale(K)[:, None]
    s2 = mx_kscale(M)[:, None]
    u = mx_kscale(H)[:, None]
    d = {}
    d["tab_words"], d["tab_scales"] = pack_weight(n((K, T)) * s, "e4m3")
    d["offs"] = striped(np.random.permutation(T)[:S])
    d["tab2_words"], d["tab2_scales"] = pack_weight(n((M, TG)) * s2, "e4m3")
    d["offs2"] = striped(np.random.permutation(TG)[:P])
    d["pos1"] = striped(np.random.permutation(S)[:P])
    d["w1_words"], d["w1_scales"] = pack_weight(n((K, H)) / s * u.T / K ** 0.5, "e2m1")
    d["b1"] = (0.5 * n(H) * u[:, 0]).astype(np.float32)
    d["w2"] = (0.45 * n((M, H)) / s2 / M ** 0.5).astype(np.float32)
    d["wgs"] = np.exp(0.3 * np.minimum(n((128, P)), 0.8)).astype(np.float32)
    d["gz"] = (1.5 * np.exp(0.3 * n(H)) * u[:, 0]).astype(np.float32)
    d["w3"] = (n((H, N)) / u / H ** 0.5 * np.exp(0.8 * n(N))[None, :]).astype(np.float32)
    return d

def reference(tab_words, tab_scales, offs, tab2_words, tab2_scales, offs2, pos1,
              w1_words, w1_scales, b1, w2, wgs, gz, w3):
    v = unpack_weight(tab_words, tab_scales, "e4m3")[:, unstriped(offs)]
    v2 = unpack_weight(tab2_words, tab2_scales, "e4m3")[:, unstriped(offs2)]
    w1 = unpack_weight(w1_words, w1_scales, "e2m1")
    a = (w1.T @ v) + f64(b1)[:, None]
    b = mxq(f64(w2), 0, "e4m3").T @ v2
    placed = np.zeros((H, S))
    placed[:, unstriped(pos1)] = np.tile(f64(wgs), (H // 128, 1)) * b
    z = a * np.cos(placed) + f64(gz)[:, None] * placed
    y = mxq(f64(w3), 0, "e4m3").T @ mxq(z, 0, "e4m3")
    words, scales = planes(y)
    return y, words, scales

@@ -1,0 +1,286 @@
+import math
+from contextlib import ExitStack
+
+import concourse.mybir as mybir
+
+T, S, TG, G, K, M, H, N = 4096, 1024, 2048, 512, 1024, 1536, 1024, 512
+FLOPS = 2 * (K * H * S + M * H * G + H * N * S)
+
+F32 = mybir.dt.float32
+BF16 = mybir.dt.bfloat16
+I32 = mybir.dt.int32
+U32 = mybir.dt.uint32
+U16 = mybir.dt.uint16
+U8 = mybir.dt.uint8
+E4M3 = mybir.dt.float8_e4m3fn_x4
+E2M1 = mybir.dt.float4_e2m1fn_x4
+ALU = mybir.AluOpType
+ACT = mybir.ActivationFunctionType
+
+P = 128
+PACK = 4
+PASS = P * PACK
+BANK = 512
+QUADS = 4
+QUAD = 32
+PAGES = 5
+RUN = 4
+QUARTER = 256
+
+
+def tile_list_race_lapping_features_kernel(
+    tc, tab_words, tab_scales, offs, tab2_words, tab2_scales, offs2, pos1,
+    w1_words, w1_scales, b1, w2, wgs, gz, w3, out_0, out_1, out_2,
+):
+    nc = tc.nc
+    k_passes, m_passes, r_passes, halves = K // PASS, M // PASS, H // PASS, S // BANK
+
+    with ExitStack() as ctx:
+        lists = ctx.enter_context(tc.tile_pool(name="lists", bufs=1))
+        keep = ctx.enter_context(tc.tile_pool(name="keep", bufs=1))
+        psum = ctx.enter_context(tc.psum_pool(name="psum", bufs=1))
+
+        def tile(shape, dtype, name, tag=None, bufs=1):
+            return keep.tile(shape, dtype, name=name, tag=tag or name, bufs=bufs, align_bytes=64)
+
+        idx = lists.tile([P, S // 16], U16, name="idx")
+        idx2 = lists.tile([P, G // 16], U16, name="idx2")
+        slot = lists.tile([P, G // 16], U16, name="slot")
+        nc.sync.dma_start(idx2[:], offs2)
+        nc.sync.dma_start(idx[:], offs)
+        nc.sync.dma_start(slot[:], pos1)
+
+        tab2_plane = tile([P, TG], U8, "tab2_plane")
+        tab_plane = tile([P, T], U8, "tab_plane")
+        w1_plane_raw = tile([P, k_passes, H], U8, "w1_plane_raw")
+        v_plane1 = tile([P, S], U8, "v_plane1")
+        nc.vector.memset(tab2_plane[:].bitcast(I32), 0)
+        nc.vector.memset(tab_plane[:].bitcast(I32), 0)
+        nc.vector.memset(w1_plane_raw[:].rearrange("p a c -> p (a c)").bitcast(I32), 0)
+        nc.vector.memset(v_plane1[:].bitcast(I32), 0)
+        pages = [tile([P, S], F32, "page%d" % i) for i in range(PAGES)]
+        for page in pages:
+            nc.vector.memset(page[:], 0.0)
+        one = tile([P, 1], F32, "one")
+        half_pi = tile([P, 1], F32, "half_pi")
+        nc.vector.memset(one[:], 1.0)
+        nc.scalar.activation(half_pi[:], one[:], ACT.Copy, scale=math.pi / 2)
+
+        def load_plane(plane, scales, passes):
+            for q in range(QUADS):
+                nc.sync.dma_start(
+                    plane[QUAD * q : QUAD * q + 4 * passes, :].bitcast(I32),
+                    scales[:, 4 * q : 4 * q + 4, :].bitcast(I32),
+                )
+
+        def load_weight(w, a, b):
+            raw = tile([P, PACK, BANK], F32, "raw", bufs=3)
+            rows = w[PASS * a : PASS * (a + 1), BANK * b : BANK * (b + 1)]
+            nc.sync.dma_start(raw[:], rows.rearrange("(p j) c -> p j c", j=PACK))
+            return raw
+
+        def quantise_weight(raw, name):
+            rounded = tile([P, BANK * PACK], BF16, "rounded", bufs=3)
+            nc.scalar.copy(
+                rounded[:].rearrange("p (t m j) -> p m j t", t=PACK, j=PACK),
+                raw[:].rearrange("p j (m t) -> p m j t", t=PACK),
+            )
+            codes = tile([P, BANK], U32, name + "_codes")
+            plane = tile([P, BANK], U8, name + "_plane")
+            nc.vector.quantize_mx(out=codes[:].bitcast(E4M3), scales=plane[:], in_=rounded[:])
+            return codes, plane
+
+        def load_table(words, a, width, tag):
+            window = tile([P, width], I32, tag)
+            nc.sync.dma_start(window[:], words[a].rearrange("p t i -> p (t i)").bitcast(I32))
+            return window
+
+        def gather(window, offsets, count, dtype, name):
+            picked = tile([P, count], dtype, name)
+            nc.vector.tensor_copy(picked[:], window[:].bitcast(dtype).indirect(offsets[:]))
+            return picked
+
+        w2_raw = {(a, 0): load_weight(w2, a, 0) for a in range(m_passes)}
+        tab2_win = [load_table(tab2_words, a, TG, "tab2_%d" % a) for a in range(m_passes - 1)]
+        load_plane(tab2_plane, tab2_scales, m_passes)
+        tab2_win.append(load_table(tab2_words, m_passes - 1, TG, "tab2_%d" % (m_passes - 1)))
+        load_plane(tab_plane, tab_scales, k_passes)
+        wgs_rows = tile([P, PACK, G], F32, "wgs_rows")
+        for q in (0, 2, 1, 3):
+            nc.sync.dma_start(
+                wgs_rows[QUAD * q : QUAD * (q + 1), :, :], wgs.rearrange("(m t) j -> m t j", t=PACK)
+            )
+        b1_col = tile([P, r_passes, PACK], F32, "b1_col")
+        gz_col = tile([P, r_passes, PACK], F32, "gz_col")
+        nc.sync.dma_start(gz_col[:], gz.rearrange("(b p t) -> p b t", p=P, t=PACK))
+        nc.sync.dma_start(b1_col[:], b1.rearrange("(b p t) -> p b t", p=P, t=PACK))
+
+        w2_q = {}
+        for a in range(m_passes):
+            w2_q[a, 0] = quantise_weight(w2_raw[a, 0], "w2_%d_0" % a)
+        v2_words = [gather(tab2_win[a], idx2, G, U32, "v2_words%d" % a) for a in range(m_passes - 1)]
+        v2_plane = gather(tab2_plane, idx2, G, U8, "v2_plane")
+        v2_words.append(gather(tab2_win[m_passes - 1], idx2, G, U32, "v2_words%d" % (m_passes - 1)))
+        v_plane0 = gather(tab_plane, idx, S, U8, "v_plane0")
+
+        for a in range(m_passes):
+            w2_raw[a, 1] = load_weight(w2, a, 1)
+        moved = QUAD * (QUADS - 1) + 4
+        nc.sync.dma_start(v_plane1[0:moved, :].bitcast(I32), v_plane0[4 : 4 + moved, :].bitcast(I32))
+        v_planes = [v_plane0, v_plane1]
+        tab_win = [load_table(tab_words, a, T, "tab_%d" % a) for a in range(k_passes)]
+        w1_raw = tile([P, k_passes, 2 * H], U8, "w1_raw")
+        nc.sync.dma_start(w1_raw[:].bitcast(I32), w1_words.rearrange("a p c -> p a c").bitcast(I32))
+        for q in range(QUADS):
+            nc.sync.dma_start(
+                w1_plane_raw[QUAD * q : QUAD * q + 4, :, :].bitcast(I32),
+                w1_scales[:, 4 * q : 4 * q + 4, :].rearrange("a r c -> r a c").bitcast(I32),
+            )
+        w3_raw = [load_weight(w3, b, 0) for b in range(r_passes)]
+
+        terms = {}
+
+        def place(b, t):
+            acc = psum.tile([P, BANK], F32, name="acc", tag="acc", bufs=3)
+            cols = slice(P * t, P * (t + 1))
+            for a in range(m_passes):
+                codes, plane = w2_q[a, b]
+                nc.tensor.matmul_mx(
+                    out=acc[:], lhsT=codes[:, cols].bitcast(E4M3), lhsT_scale=plane[:, cols],
+                    rhs=v2_words[a][:].bitcast(E4M3), rhs_scale=v2_plane[4 * a : P, :],
+                    start=(a == 0), stop=(a == m_passes - 1),
+                )
+            offsets = tile([P, G], F32, "offsets", bufs=4)
+            nc.scalar.copy(offsets[:], acc[:])
+            page = pages[(PACK * b + t) % PAGES]
+            nc.vector.tensor_tensor(page[:].indirect(slot[:]), offsets[:], wgs_rows[:, t, :], ALU.mult)
+
+        def read_page(b, t):
+            page = pages[(PACK * b + t) % PAGES]
+            size = tile([P, S], F32, "size", bufs=2)
+            nc.scalar.activation(size[:], page[:], ACT.Abs)
+            for h in range(halves):
+                js = slice(BANK * h, BANK * (h + 1))
+                nc.scalar.activation(terms[b, h][:, 1, t, :], page[:, js], ACT.Copy, scale=gz_col[:, b, t : t + 1])
+            for h in range(halves):
+                js = slice(BANK * h, BANK * (h + 1))
+                nc.scalar.activation(terms[b, h][:, 0, t, :], size[:, js], ACT.Sin, bias=half_pi[:], scale=-1.0)
+
+        for h in range(halves):
+            terms[0, h] = tile([P, 2, PACK, BANK], F32, "terms0_%d" % h)
+        for t in range(PACK):
+            place(0, t)
+        for a in range(m_passes):
+            w2_q[a, 1] = quantise_weight(w2_raw[a, 1], "w2_%d_1" % a)
+        place(1, 0)
+        for t in range(PACK):
+            read_page(0, t)
+            if t + 1 < PACK:
+                place(1, t + 1)
+
+        v_words = [gather(tab_win[a], idx, S, U32, "v_words%d" % a) for a in range(k_passes)]
+        w1_codes = tile([P, k_passes, 2 * H], U8, "w1_codes")
+        nc.scalar.copy(
+            w1_codes[:].bitcast(U16).rearrange("p a (b t m) -> p (a b) t m", t=PACK, m=P),
+            w1_raw[:].bitcast(U16).rearrange("p a (b m t) -> p (a b) t m", t=PACK, m=P),
+        )
+        w1_plane = tile([P, k_passes, H], U8, "w1_plane")
+        nc.vector.tensor_copy(
+            w1_plane[:].rearrange("p a (b t m) -> p (a b) t m", t=PACK, m=P),
+            w1_plane_raw[:].rearrange("p a (b m t) -> p (a b) t m", t=PACK, m=P),
+        )
+
+        def modulate(b, t, h):
+            acc = psum.tile([P, BANK], F32, name="acc", tag="acc", bufs=3)
+            first = BANK * b + P * t
+            js = slice(BANK * h, BANK * (h + 1))
+            for a in range(k_passes):
+                nc.tensor.matmul_mx(
+                    out=acc[:],
+                    lhsT=w1_codes[:, a, 2 * first : 2 * (first + P)].bitcast(E2M1),
+                    lhsT_scale=w1_plane[:, a, first : first + P],
+                    rhs=v_words[a][:, js].bitcast(E4M3), rhs_scale=v_planes[a][:, js],
+                    start=(a == 0), stop=(a == k_passes - 1),
+                )
+            cosine = terms[b, h][:, 0, t, :]
+            nc.vector.scalar_tensor_tensor(cosine, acc[:], b1_col[:, b, t : t + 1], cosine, ALU.add, ALU.mult)
+
+        z_codes = {(b, h): tile([P, BANK], U32, "z_codes%d%d" % (b, h)) for b in range(r_passes) for h in range(halves)}
+        z_plane = {(b, h): tile([P, BANK], U8, "z_plane%d%d" % (b, h)) for b in range(r_passes) for h in range(halves)}
+
+        def join(b, h, js):
+            width = js.stop - js.start
+            rounded = tile([P, width * PACK], BF16, "rounded", bufs=3)
+            walk = "p t (c i) -> p c t i"
+            nc.vector.tensor_tensor(
+                rounded[:].rearrange("p (c i t) -> p c t i", i=RUN, t=PACK),
+                terms[b, h][:, 0, :, js].rearrange(walk, i=RUN),
+                terms[b, h][:, 1, :, js].rearrange(walk, i=RUN),
+                ALU.add,
+            )
+            return rounded
+
+        def quantise_z(b, h, js, rounded):
+            nc.vector.quantize_mx(out=z_codes[b, h][:, js].bitcast(E4M3), scales=z_plane[b, h][:, js], in_=rounded[:])
+
+        whole = slice(0, BANK)
+        for h in range(halves):
+            terms[1, h] = tile([P, 2, PACK, BANK], F32, "terms1_%d" % h, tag="tab_%d" % h)
+        for t in range(PACK):
+            read_page(1, t)
+        for h in range(halves):
+            for t in range(PACK):
+                modulate(0, t, h)
+        z_bf = [join(0, h, whole) for h in range(halves)]
+        for h in range(halves):
+            quantise_z(0, h, whole, z_bf[h])
+        w3_q = [quantise_weight(w3_raw[b], "w2_%d_0" % b) for b in range(r_passes)]
+
+        y_codes = tile([P, S], U32, "y_codes")
+        y_plane = tile([P, S], U8, "y_plane")
+        out_rows = out_0.rearrange("(p t) j -> p t j", t=PACK)
+        out_words = out_1[0].rearrange("p m t -> p (m t)").bitcast(I32)
+
+        def project(u):
+            y = tile([P, PACK, QUARTER], F32, "y", tag="raw", bufs=3)
+            rounded = tile([P, QUARTER * PACK], BF16, "y_rounded", bufs=2)
+            h = QUARTER * u // BANK
+            for c in range(QUARTER // P):
+                acc = psum.tile([P, PACK, P], F32, name="y_acc", tag="y_acc", bufs=5)
+                first = QUARTER * u + P * c - BANK * h
+                js = slice(first, first + P)
+                for b in range(r_passes):
+                    for t in range(PACK):
+                        cols = slice(P * t, P * (t + 1))
+                        nc.tensor.matmul_mx(
+                            out=acc[:, t, :], lhsT=w3_q[b][0][:, cols].bitcast(E4M3), lhsT_scale=w3_q[b][1][:, cols],
+                            rhs=z_codes[b, h][:, js].bitcast(E4M3), rhs_scale=z_plane[b, h][:, js],
+                            start=(b == 0 and t == 0), stop=(b == r_passes - 1 and t == PACK - 1),
+                        )
+                nc.scalar.copy(y[:, :, P * c : P * (c + 1)], acc[:])
+                woven = rounded[:, PACK * P * c : PACK * P * (c + 1)].rearrange("p (j t) -> p j t", t=PACK)
+                if h == 0:
+                    nc.scalar.copy(woven, acc[:].rearrange("p t j -> p j t"))
+                else:
+                    nc.vector.tensor_copy(woven, acc[:].rearrange("p t j -> p j t"))
+            js = slice(QUARTER * u, QUARTER * (u + 1))
+            nc.sync.dma_start(out_rows[:, :, js], y[:])
+            nc.vector.quantize_mx(out=y_codes[:, js].bitcast(E4M3), scales=y_plane[:, js], in_=rounded[:])
+            nc.sync.dma_start(out_words[:, js], y_codes[:, js].bitcast(I32))
+
+        for t in range(PACK):
+            modulate(1, t, 0)
+        rounded = join(1, 0, whole)
+        for t in range(PACK):
+            modulate(1, t, 1)
+            if t == 0:
+                quantise_z(1, 0, whole, rounded)
+        parts = [slice(QUARTER * u, QUARTER * (u + 1)) for u in range(BANK // QUARTER)]
+        z_bf = [join(1, 1, js) for js in parts]
+        for js, rounded in zip(parts, z_bf):
+            quantise_z(1, 1, js, rounded)
+        for u in range(S // QUARTER):
+            project(u)
+        for q in range(QUADS):
+            queue = nc.scalar if q % 2 else nc.sync
+            queue.dma_start(out_2[0, 4 * q : 4 * q + 4, :].bitcast(I32), y_plane[QUAD * q : QUAD * q + 4, :].bitcast(I32))

@@ -2,6 +2,7 @@ import math
 from contextlib import ExitStack
 
 import concourse.mybir as mybir
+from concourse.masks import make_identity
 
 T, S, TG, G, K, M, H, N = 4096, 1024, 2048, 512, 1024, 1536, 1024, 512
 FLOPS = 2 * (K * H * S + M * H * G + H * N * S)
@@ -23,7 +24,6 @@ PASS = P * PACK
 BANK = 512
 QUADS = 4
 QUAD = 32
-PAGES = 5
 RUN = 4
 QUARTER = 256
 
@@ -43,12 +43,17 @@ def tile_list_race_lapping_features_kernel(
         def tile(shape, dtype, name, tag=None, bufs=1):
             return keep.tile(shape, dtype, name=name, tag=tag or name, bufs=bufs, align_bytes=64)
 
+        def bank(shape, tag):
+            return psum.tile(shape, F32, name=tag, tag=tag, bufs={"acc": 4, "wide": 4}[tag])
+
         idx = lists.tile([P, S // 16], U16, name="idx")
         idx2 = lists.tile([P, G // 16], U16, name="idx2")
         slot = lists.tile([P, G // 16], U16, name="slot")
         nc.sync.dma_start(idx2[:], offs2)
         nc.sync.dma_start(idx[:], offs)
         nc.sync.dma_start(slot[:], pos1)
+        wgs_raw = tile([P, G], F32, "wgs_raw")
+        nc.sync.dma_start(wgs_raw[:], wgs)
 
         tab2_plane = tile([P, TG], U8, "tab2_plane")
         tab_plane = tile([P, T], U8, "tab_plane")
@@ -58,9 +63,8 @@ def tile_list_race_lapping_features_kernel(
         nc.vector.memset(tab_plane[:].bitcast(I32), 0)
         nc.vector.memset(w1_plane_raw[:].rearrange("p a c -> p (a c)").bitcast(I32), 0)
         nc.vector.memset(v_plane1[:].bitcast(I32), 0)
-        pages = [tile([P, S], F32, "page%d" % i) for i in range(PAGES)]
-        for page in pages:
-            nc.vector.memset(page[:], 0.0)
+        identity = tile([P, P], F32, "identity")
+        make_identity(nc, identity[:])
         one = tile([P, 1], F32, "one")
         half_pi = tile([P, 1], F32, "half_pi")
         nc.vector.memset(one[:], 1.0)
@@ -68,7 +72,7 @@ def tile_list_race_lapping_features_kernel(
 
         def load_plane(plane, scales, passes):
             for q in range(QUADS):
-                nc.sync.dma_start(
+                nc.gpsimd.dma_start(
                     plane[QUAD * q : QUAD * q + 4 * passes, :].bitcast(I32),
                     scales[:, 4 * q : 4 * q + 4, :].bitcast(I32),
                 )
@@ -101,47 +105,61 @@ def tile_list_race_lapping_features_kernel(
             return picked
 
         w2_raw = {(a, 0): load_weight(w2, a, 0) for a in range(m_passes)}
-        tab2_win = [load_table(tab2_words, a, TG, "tab2_%d" % a) for a in range(m_passes - 1)]
         load_plane(tab2_plane, tab2_scales, m_passes)
-        tab2_win.append(load_table(tab2_words, m_passes - 1, TG, "tab2_%d" % (m_passes - 1)))
+        tab2_win = [load_table(tab2_words, a, TG, "tab2_%d" % a) for a in range(m_passes)]
         load_plane(tab_plane, tab_scales, k_passes)
-        wgs_rows = tile([P, PACK, G], F32, "wgs_rows")
-        for q in (0, 2, 1, 3):
-            nc.sync.dma_start(
-                wgs_rows[QUAD * q : QUAD * (q + 1), :, :], wgs.rearrange("(m t) j -> m t j", t=PACK)
+        for q in range(QUADS):
+            nc.gpsimd.dma_start(
+                w1_plane_raw[QUAD * q : QUAD * q + 4, :, :].bitcast(I32),
+                w1_scales[:, 4 * q : 4 * q + 4, :].rearrange("a r c -> r a c").bitcast(I32),
             )
         b1_col = tile([P, r_passes, PACK], F32, "b1_col")
         gz_col = tile([P, r_passes, PACK], F32, "gz_col")
-        nc.sync.dma_start(gz_col[:], gz.rearrange("(b p t) -> p b t", p=P, t=PACK))
-        nc.sync.dma_start(b1_col[:], b1.rearrange("(b p t) -> p b t", p=P, t=PACK))
+        pages = {(b, t): tile([P, S], F32, "page%d%d" % (b, t)) for b in range(r_passes) for t in range(PACK)}
+        for page in [pages[key] for key in pages]:
+            nc.gpsimd.memset(page[:], 0.0)
+
+        turned = bank([P, G // P, P], "wide")
+        for jb in range(G // P):
+            nc.tensor.transpose(turned[:, jb, :], wgs_raw[:, P * jb : P * (jb + 1)], identity[:])
+        wgs_cols = tile([P, G // P, PACK, QUADS, QUAD], F32, "wgs_cols", tag="cosine0")
+        for q in range(QUADS):
+            nc.scalar.copy(wgs_cols[:, :, :, q, :], turned[:].rearrange("p b (m t) -> p b t m", t=PACK))
+        wgs_rows = tile([P, PACK, G], F32, "wgs_rows")
+        for t in range(PACK):
+            back = bank([P, G // P, P], "wide")
+            for jb in range(G // P):
+                nc.tensor.transpose(
+                    back[:, jb, :], wgs_cols[:, jb, t, :, :].rearrange("p q m -> p (q m)"), identity[:]
+                )
+            nc.scalar.copy(wgs_rows[:, t, :], back[:].rearrange("p b j -> p (b j)"))
 
         w2_q = {}
         for a in range(m_passes):
             w2_q[a, 0] = quantise_weight(w2_raw[a, 0], "w2_%d_0" % a)
-        v2_words = [gather(tab2_win[a], idx2, G, U32, "v2_words%d" % a) for a in range(m_passes - 1)]
         v2_plane = gather(tab2_plane, idx2, G, U8, "v2_plane")
-        v2_words.append(gather(tab2_win[m_passes - 1], idx2, G, U32, "v2_words%d" % (m_passes - 1)))
+        v2_words = [gather(tab2_win[a], idx2, G, U32, "v2_words%d" % a) for a in range(m_passes)]
         v_plane0 = gather(tab_plane, idx, S, U8, "v_plane0")
+        w1_plane = tile([P, k_passes, H], U8, "w1_plane")
+        nc.vector.tensor_copy(
+            w1_plane[:].rearrange("p a (b t m) -> p (a b) t m", t=PACK, m=P),
+            w1_plane_raw[:].rearrange("p a (b m t) -> p (a b) t m", t=PACK, m=P),
+        )
 
         for a in range(m_passes):
             w2_raw[a, 1] = load_weight(w2, a, 1)
-        moved = QUAD * (QUADS - 1) + 4
-        nc.sync.dma_start(v_plane1[0:moved, :].bitcast(I32), v_plane0[4 : 4 + moved, :].bitcast(I32))
-        v_planes = [v_plane0, v_plane1]
         tab_win = [load_table(tab_words, a, T, "tab_%d" % a) for a in range(k_passes)]
+        nc.sync.dma_start(gz_col[:], gz.rearrange("(b p t) -> p b t", p=P, t=PACK))
+        nc.sync.dma_start(b1_col[:], b1.rearrange("(b p t) -> p b t", p=P, t=PACK))
+        moved = QUAD * (QUADS - 1) + 4
+        nc.gpsimd.dma_start(v_plane1[0:moved, :].bitcast(I32), v_plane0[4 : 4 + moved, :].bitcast(I32))
+        v_planes = [v_plane0, v_plane1]
         w1_raw = tile([P, k_passes, 2 * H], U8, "w1_raw")
         nc.sync.dma_start(w1_raw[:].bitcast(I32), w1_words.rearrange("a p c -> p a c").bitcast(I32))
-        for q in range(QUADS):
-            nc.sync.dma_start(
-                w1_plane_raw[QUAD * q : QUAD * q + 4, :, :].bitcast(I32),
-                w1_scales[:, 4 * q : 4 * q + 4, :].rearrange("a r c -> r a c").bitcast(I32),
-            )
         w3_raw = [load_weight(w3, b, 0) for b in range(r_passes)]
 
-        terms = {}
-
         def place(b, t):
-            acc = psum.tile([P, BANK], F32, name="acc", tag="acc", bufs=3)
+            acc = bank([P, BANK], "acc")
             cols = slice(P * t, P * (t + 1))
             for a in range(m_passes):
                 codes, plane = w2_q[a, b]
@@ -152,31 +170,22 @@ def tile_list_race_lapping_features_kernel(
                 )
             offsets = tile([P, G], F32, "offsets", bufs=4)
             nc.scalar.copy(offsets[:], acc[:])
-            page = pages[(PACK * b + t) % PAGES]
-            nc.vector.tensor_tensor(page[:].indirect(slot[:]), offsets[:], wgs_rows[:, t, :], ALU.mult)
+            nc.vector.tensor_tensor(pages[b, t][:].indirect(slot[:]), offsets[:], wgs_rows[:, t, :], ALU.mult)
 
-        def read_page(b, t):
-            page = pages[(PACK * b + t) % PAGES]
+        def take_cosine(b, t):
             size = tile([P, S], F32, "size", bufs=2)
-            nc.scalar.activation(size[:], page[:], ACT.Abs)
-            for h in range(halves):
-                js = slice(BANK * h, BANK * (h + 1))
-                nc.scalar.activation(terms[b, h][:, 1, t, :], page[:, js], ACT.Copy, scale=gz_col[:, b, t : t + 1])
-            for h in range(halves):
-                js = slice(BANK * h, BANK * (h + 1))
-                nc.scalar.activation(terms[b, h][:, 0, t, :], size[:, js], ACT.Sin, bias=half_pi[:], scale=-1.0)
+            nc.scalar.activation(size[:], pages[b, t][:], ACT.Abs)
+            nc.scalar.activation(cosines[b][:, t, :], size[:], ACT.Sin, bias=half_pi[:], scale=-1.0)
 
-        for h in range(halves):
-            terms[0, h] = tile([P, 2, PACK, BANK], F32, "terms0_%d" % h)
         for t in range(PACK):
             place(0, t)
         for a in range(m_passes):
             w2_q[a, 1] = quantise_weight(w2_raw[a, 1], "w2_%d_1" % a)
-        place(1, 0)
+        cosines = [tile([P, PACK, S], F32, "cosine0")]
         for t in range(PACK):
-            read_page(0, t)
-            if t + 1 < PACK:
-                place(1, t + 1)
+            place(1, t)
+        for t in range(PACK):
+            take_cosine(0, t)
 
         v_words = [gather(tab_win[a], idx, S, U32, "v_words%d" % a) for a in range(k_passes)]
         w1_codes = tile([P, k_passes, 2 * H], U8, "w1_codes")
@@ -184,16 +193,16 @@ def tile_list_race_lapping_features_kernel(
             w1_codes[:].bitcast(U16).rearrange("p a (b t m) -> p (a b) t m", t=PACK, m=P),
             w1_raw[:].bitcast(U16).rearrange("p a (b m t) -> p (a b) t m", t=PACK, m=P),
         )
-        w1_plane = tile([P, k_passes, H], U8, "w1_plane")
-        nc.vector.tensor_copy(
-            w1_plane[:].rearrange("p a (b t m) -> p (a b) t m", t=PACK, m=P),
-            w1_plane_raw[:].rearrange("p a (b m t) -> p (a b) t m", t=PACK, m=P),
-        )
+        w3_q = [quantise_weight(w3_raw[b], "w2_%d_0" % b) for b in range(r_passes)]
+        cosines.append(tile([P, PACK, S], F32, "cosine1", tag="tab_0"))
+        for t in range(PACK):
+            take_cosine(1, t)
 
-        def modulate(b, t, h):
-            acc = psum.tile([P, BANK], F32, name="acc", tag="acc", bufs=3)
+        z_rows = tile([P, r_passes, PACK, S], BF16, "z_rows", tag="tab_1")
+
+        def modulate(b, t, js):
+            acc = bank([P, js.stop - js.start], "acc")
             first = BANK * b + P * t
-            js = slice(BANK * h, BANK * (h + 1))
             for a in range(k_passes):
                 nc.tensor.matmul_mx(
                     out=acc[:],
@@ -202,39 +211,30 @@ def tile_list_race_lapping_features_kernel(
                     rhs=v_words[a][:, js].bitcast(E4M3), rhs_scale=v_planes[a][:, js],
                     start=(a == 0), stop=(a == k_passes - 1),
                 )
-            cosine = terms[b, h][:, 0, t, :]
+            cosine = cosines[b][:, t, js]
             nc.vector.scalar_tensor_tensor(cosine, acc[:], b1_col[:, b, t : t + 1], cosine, ALU.add, ALU.mult)
 
-        z_codes = {(b, h): tile([P, BANK], U32, "z_codes%d%d" % (b, h)) for b in range(r_passes) for h in range(halves)}
-        z_plane = {(b, h): tile([P, BANK], U8, "z_plane%d%d" % (b, h)) for b in range(r_passes) for h in range(halves)}
-
-        def join(b, h, js):
-            width = js.stop - js.start
-            rounded = tile([P, width * PACK], BF16, "rounded", bufs=3)
-            walk = "p t (c i) -> p c t i"
-            nc.vector.tensor_tensor(
-                rounded[:].rearrange("p (c i t) -> p c t i", i=RUN, t=PACK),
-                terms[b, h][:, 0, :, js].rearrange(walk, i=RUN),
-                terms[b, h][:, 1, :, js].rearrange(walk, i=RUN),
-                ALU.add,
+        def join(b, t, js):
+            nc.vector.scalar_tensor_tensor(
+                z_rows[:, b, t, js], pages[b, t][:, js], gz_col[:, b, t : t + 1], cosines[b][:, t, js],
+                ALU.mult, ALU.add,
             )
-            return rounded
 
-        def quantise_z(b, h, js, rounded):
-            nc.vector.quantize_mx(out=z_codes[b, h][:, js].bitcast(E4M3), scales=z_plane[b, h][:, js], in_=rounded[:])
+        z_codes = [tile([P, S], U32, "z_codes%d" % b) for b in range(r_passes)]
+        z_plane = [tile([P, S], U8, "z_plane%d" % b) for b in range(r_passes)]
 
-        whole = slice(0, BANK)
-        for h in range(halves):
-            terms[1, h] = tile([P, 2, PACK, BANK], F32, "terms1_%d" % h, tag="tab_%d" % h)
-        for t in range(PACK):
-            read_page(1, t)
-        for h in range(halves):
-            for t in range(PACK):
-                modulate(0, t, h)
-        z_bf = [join(0, h, whole) for h in range(halves)]
-        for h in range(halves):
-            quantise_z(0, h, whole, z_bf[h])
-        w3_q = [quantise_weight(w3_raw[b], "w2_%d_0" % b) for b in range(r_passes)]
+        def make_z(b, js, copy):
+            for t in range(PACK + 1):
+                if t < PACK:
+                    modulate(b, t, js)
+                if t > 0:
+                    join(b, t - 1, js)
+            woven = tile([P, (js.stop - js.start) * PACK], BF16, "rounded", bufs=3)
+            copy(
+                woven[:].rearrange("p (c i t) -> p c t i", i=RUN, t=PACK),
+                z_rows[:, b, :, js].rearrange("p t (c i) -> p c t i", i=RUN),
+            )
+            nc.vector.quantize_mx(out=z_codes[b][:, js].bitcast(E4M3), scales=z_plane[b][:, js], in_=woven[:])
 
         y_codes = tile([P, S], U32, "y_codes")
         y_plane = tile([P, S], U8, "y_plane")
@@ -246,15 +246,15 @@ def tile_list_race_lapping_features_kernel(
             rounded = tile([P, QUARTER * PACK], BF16, "y_rounded", bufs=2)
             h = QUARTER * u // BANK
             for c in range(QUARTER // P):
-                acc = psum.tile([P, PACK, P], F32, name="y_acc", tag="y_acc", bufs=5)
-                first = QUARTER * u + P * c - BANK * h
+                acc = bank([P, PACK, P], "wide")
+                first = QUARTER * u + P * c
                 js = slice(first, first + P)
                 for b in range(r_passes):
                     for t in range(PACK):
                         cols = slice(P * t, P * (t + 1))
                         nc.tensor.matmul_mx(
                             out=acc[:, t, :], lhsT=w3_q[b][0][:, cols].bitcast(E4M3), lhsT_scale=w3_q[b][1][:, cols],
-                            rhs=z_codes[b, h][:, js].bitcast(E4M3), rhs_scale=z_plane[b, h][:, js],
+                            rhs=z_codes[b][:, js].bitcast(E4M3), rhs_scale=z_plane[b][:, js],
                             start=(b == 0 and t == 0), stop=(b == r_passes - 1 and t == PACK - 1),
                         )
                 nc.scalar.copy(y[:, :, P * c : P * (c + 1)], acc[:])
@@ -268,19 +268,15 @@ def tile_list_race_lapping_features_kernel(
             nc.vector.quantize_mx(out=y_codes[:, js].bitcast(E4M3), scales=y_plane[:, js], in_=rounded[:])
             nc.sync.dma_start(out_words[:, js], y_codes[:, js].bitcast(I32))
 
-        for t in range(PACK):
-            modulate(1, t, 0)
-        rounded = join(1, 0, whole)
-        for t in range(PACK):
-            modulate(1, t, 1)
-            if t == 0:
-                quantise_z(1, 0, whole, rounded)
-        parts = [slice(QUARTER * u, QUARTER * (u + 1)) for u in range(BANK // QUARTER)]
-        z_bf = [join(1, 1, js) for js in parts]
-        for js, rounded in zip(parts, z_bf):
-            quantise_z(1, 1, js, rounded)
-        for u in range(S // QUARTER):
-            project(u)
+        make_z(0, slice(0, BANK), nc.scalar.copy)
+        make_z(1, slice(0, BANK), nc.scalar.copy)
+        make_z(0, slice(BANK, S), nc.scalar.copy)
+        project(0)
+        project(1)
+        make_z(1, slice(BANK, BANK + QUARTER), nc.vector.tensor_copy)
+        make_z(1, slice(BANK + QUARTER, S), nc.vector.tensor_copy)
+        project(2)
+        project(3)
         for q in range(QUADS):
             queue = nc.scalar if q % 2 else nc.sync
             queue.dma_start(out_2[0, 4 * q : 4 * q + 4, :].bitcast(I32), y_plane[QUAD * q : QUAD * q + 4, :].bitcast(I32))

@@ -83,9 +83,9 @@ def tile_list_race_lapping_features_kernel(
             nc.sync.dma_start(raw[:], rows.rearrange("(p j) c -> p j c", j=PACK))
             return raw
 
-        def quantise_weight(raw, name):
+        def quantise_weight(raw, name, copy):
             rounded = tile([P, BANK * PACK], BF16, "rounded", bufs=3)
-            nc.scalar.copy(
+            copy(
                 rounded[:].rearrange("p (t m j) -> p m j t", t=PACK, j=PACK),
                 raw[:].rearrange("p j (m t) -> p m j t", t=PACK),
             )
@@ -109,15 +109,22 @@ def tile_list_race_lapping_features_kernel(
         tab2_win = [load_table(tab2_words, a, TG, "tab2_%d" % a) for a in range(m_passes)]
         load_plane(tab_plane, tab_scales, k_passes)
         for q in range(QUADS):
-            nc.gpsimd.dma_start(
+            nc.scalar.dma_start(
                 w1_plane_raw[QUAD * q : QUAD * q + 4, :, :].bitcast(I32),
                 w1_scales[:, 4 * q : 4 * q + 4, :].rearrange("a r c -> r a c").bitcast(I32),
             )
         b1_col = tile([P, r_passes, PACK], F32, "b1_col")
         gz_col = tile([P, r_passes, PACK], F32, "gz_col")
-        pages = {(b, t): tile([P, S], F32, "page%d%d" % (b, t)) for b in range(r_passes) for t in range(PACK)}
-        for page in [pages[key] for key in pages]:
-            nc.gpsimd.memset(page[:], 0.0)
+        pages = {}
+
+        def open_page(b, t, tag=None):
+            pages[b, t] = tile([P, S], F32, "page%d%d" % (b, t), tag=tag)
+            nc.gpsimd.memset(pages[b, t][:], 0.0)
+
+        early = [(b, t) for b in range(r_passes) for t in range(PACK)][:-k_passes]
+        late = [(r_passes - 1, PACK - k_passes + a) for a in range(k_passes)]
+        for b, t in early:
+            open_page(b, t)
 
         turned = bank([P, G // P, P], "wide")
         for jb in range(G // P):
@@ -136,7 +143,7 @@ def tile_list_race_lapping_features_kernel(
 
         w2_q = {}
         for a in range(m_passes):
-            w2_q[a, 0] = quantise_weight(w2_raw[a, 0], "w2_%d_0" % a)
+            w2_q[a, 0] = quantise_weight(w2_raw[a, 0], "w2_%d_0" % a, nc.vector.tensor_copy if a == m_passes - 1 else nc.scalar.copy)
         v2_plane = gather(tab2_plane, idx2, G, U8, "v2_plane")
         v2_words = [gather(tab2_win[a], idx2, G, U32, "v2_words%d" % a) for a in range(m_passes)]
         v_plane0 = gather(tab_plane, idx, S, U8, "v_plane0")
@@ -175,30 +182,37 @@ def tile_list_race_lapping_features_kernel(
         def take_cosine(b, t):
             size = tile([P, S], F32, "size", bufs=2)
             nc.scalar.activation(size[:], pages[b, t][:], ACT.Abs)
-            nc.scalar.activation(cosines[b][:, t, :], size[:], ACT.Sin, bias=half_pi[:], scale=-1.0)
+            nc.scalar.activation(cosines[b, t], size[:], ACT.Sin, bias=half_pi[:], scale=-1.0)
 
         for t in range(PACK):
             place(0, t)
         for a in range(m_passes):
-            w2_q[a, 1] = quantise_weight(w2_raw[a, 1], "w2_%d_1" % a)
-        cosines = [tile([P, PACK, S], F32, "cosine0")]
-        for t in range(PACK):
-            place(1, t)
+            w2_q[a, 1] = quantise_weight(w2_raw[a, 1], "w2_%d_1" % a, nc.scalar.copy)
+        cosine0 = tile([P, PACK, S], F32, "cosine0")
+        cosines = {(0, t): cosine0[:, t, :] for t in range(PACK)}
+        for b, t in early[PACK:]:
+            place(b, t)
         for t in range(PACK):
             take_cosine(0, t)
 
         v_words = [gather(tab_win[a], idx, S, U32, "v_words%d" % a) for a in range(k_passes)]
+        for a, (b, t) in enumerate(late):
+            open_page(b, t, tag="tab_%d" % a)
+            place(b, t)
         w1_codes = tile([P, k_passes, 2 * H], U8, "w1_codes")
         nc.scalar.copy(
             w1_codes[:].bitcast(U16).rearrange("p a (b t m) -> p (a b) t m", t=PACK, m=P),
             w1_raw[:].bitcast(U16).rearrange("p a (b m t) -> p (a b) t m", t=PACK, m=P),
         )
-        w3_q = [quantise_weight(w3_raw[b], "w2_%d_0" % b) for b in range(r_passes)]
-        cosines.append(tile([P, PACK, S], F32, "cosine1", tag="tab_0"))
+        w3_q = [quantise_weight(w3_raw[b], "w2_%d_0" % b, nc.scalar.copy) for b in range(r_passes)]
+        for pair, tag in enumerate(("tab2_2", "cosine1")):
+            cosine1 = tile([P, 2, S], F32, "cosine1_%d" % pair, tag=tag)
+            for e in range(2):
+                cosines[1, 2 * pair + e] = cosine1[:, e, :]
         for t in range(PACK):
             take_cosine(1, t)
 
-        z_rows = tile([P, r_passes, PACK, S], BF16, "z_rows", tag="tab_1")
+        z_rows = [tile([P, PACK, S], BF16, "z_rows%d" % b, tag="tab2_%d" % b) for b in range(r_passes)]
 
         def modulate(b, t, js):
             acc = bank([P, js.stop - js.start], "acc")
@@ -211,12 +225,12 @@ def tile_list_race_lapping_features_kernel(
                     rhs=v_words[a][:, js].bitcast(E4M3), rhs_scale=v_planes[a][:, js],
                     start=(a == 0), stop=(a == k_passes - 1),
                 )
-            cosine = cosines[b][:, t, js]
+            cosine = cosines[b, t][:, js]
             nc.vector.scalar_tensor_tensor(cosine, acc[:], b1_col[:, b, t : t + 1], cosine, ALU.add, ALU.mult)
 
         def join(b, t, js):
             nc.vector.scalar_tensor_tensor(
-                z_rows[:, b, t, js], pages[b, t][:, js], gz_col[:, b, t : t + 1], cosines[b][:, t, js],
+                z_rows[b][:, t, js], pages[b, t][:, js], gz_col[:, b, t : t + 1], cosines[b, t][:, js],
                 ALU.mult, ALU.add,
             )
 
@@ -232,7 +246,7 @@ def tile_list_race_lapping_features_kernel(
             woven = tile([P, (js.stop - js.start) * PACK], BF16, "rounded", bufs=3)
             copy(
                 woven[:].rearrange("p (c i t) -> p c t i", i=RUN, t=PACK),
-                z_rows[:, b, :, js].rearrange("p t (c i) -> p c t i", i=RUN),
+                z_rows[b][:, :, js].rearrange("p t (c i) -> p c t i", i=RUN),
             )
             nc.vector.quantize_mx(out=z_codes[b][:, js].bitcast(E4M3), scales=z_plane[b][:, js], in_=woven[:])
 
@@ -244,7 +258,6 @@ def tile_list_race_lapping_features_kernel(
         def project(u):
             y = tile([P, PACK, QUARTER], F32, "y", tag="raw", bufs=3)
             rounded = tile([P, QUARTER * PACK], BF16, "y_rounded", bufs=2)
-            h = QUARTER * u // BANK
             for c in range(QUARTER // P):
                 acc = bank([P, PACK, P], "wide")
                 first = QUARTER * u + P * c
@@ -259,7 +272,7 @@ def tile_list_race_lapping_features_kernel(
                         )
                 nc.scalar.copy(y[:, :, P * c : P * (c + 1)], acc[:])
                 woven = rounded[:, PACK * P * c : PACK * P * (c + 1)].rearrange("p (j t) -> p j t", t=PACK)
-                if h == 0:
+                if u < S // QUARTER - 1:
                     nc.scalar.copy(woven, acc[:].rearrange("p t j -> p j t"))
                 else:
                     nc.vector.tensor_copy(woven, acc[:].rearrange("p t j -> p j t"))

@@ -86,8 +86,8 @@ def tile_list_race_lapping_features_kernel(
         def quantise_weight(raw, name, copy):
             rounded = tile([P, BANK * PACK], BF16, "rounded", bufs=3)
             copy(
-                rounded[:].rearrange("p (t m j) -> p m j t", t=PACK, j=PACK),
-                raw[:].rearrange("p j (m t) -> p m j t", t=PACK),
+                rounded[:].rearrange("p (u e m j) -> p u m j e", u=2, e=2, j=PACK),
+                raw[:].rearrange("p j (m u e) -> p u m j e", u=2, e=2),
             )
             codes = tile([P, BANK], U32, name + "_codes")
             plane = tile([P, BANK], U8, name + "_plane")

import math
from contextlib import ExitStack

import concourse.mybir as mybir
from concourse.masks import make_identity

T, S, TG, G, K, M, H, N = 4096, 1024, 2048, 512, 1024, 1536, 1024, 512
FLOPS = 2 * (K * H * S + M * H * G + H * N * S)

F32 = mybir.dt.float32
BF16 = mybir.dt.bfloat16
I32 = mybir.dt.int32
U32 = mybir.dt.uint32
U16 = mybir.dt.uint16
U8 = mybir.dt.uint8
E4M3 = mybir.dt.float8_e4m3fn_x4
E2M1 = mybir.dt.float4_e2m1fn_x4
ALU = mybir.AluOpType
ACT = mybir.ActivationFunctionType

P = 128
PACK = 4
PASS = P * PACK
BANK = 512
QUADS = 4
QUAD = 32
RUN = 4
QUARTER = 256


def tile_list_race_lapping_features_kernel(
    tc, tab_words, tab_scales, offs, tab2_words, tab2_scales, offs2, pos1,
    w1_words, w1_scales, b1, w2, wgs, gz, w3, out_0, out_1, out_2,
):
    nc = tc.nc
    k_passes, m_passes, r_passes, halves = K // PASS, M // PASS, H // PASS, S // BANK

    with ExitStack() as ctx:
        lists = ctx.enter_context(tc.tile_pool(name="lists", bufs=1))
        keep = ctx.enter_context(tc.tile_pool(name="keep", bufs=1))
        psum = ctx.enter_context(tc.psum_pool(name="psum", bufs=1))

        def tile(shape, dtype, name, tag=None, bufs=1):
            return keep.tile(shape, dtype, name=name, tag=tag or name, bufs=bufs, align_bytes=64)

        def bank(shape, tag):
            return psum.tile(shape, F32, name=tag, tag=tag, bufs={"acc": 4, "wide": 4}[tag])

        idx = lists.tile([P, S // 16], U16, name="idx")
        idx2 = lists.tile([P, G // 16], U16, name="idx2")
        slot = lists.tile([P, G // 16], U16, name="slot")
        nc.sync.dma_start(idx2[:], offs2)
        nc.sync.dma_start(idx[:], offs)
        nc.sync.dma_start(slot[:], pos1)
        wgs_raw = tile([P, G], F32, "wgs_raw")
        nc.sync.dma_start(wgs_raw[:], wgs)

        tab2_plane = tile([P, TG], U8, "tab2_plane")
        tab_plane = tile([P, T], U8, "tab_plane")
        w1_plane_raw = tile([P, k_passes, H], U8, "w1_plane_raw")
        v_plane1 = tile([P, S], U8, "v_plane1")
        nc.vector.memset(tab2_plane[:].bitcast(I32), 0)
        nc.vector.memset(tab_plane[:].bitcast(I32), 0)
        nc.vector.memset(w1_plane_raw[:].rearrange("p a c -> p (a c)").bitcast(I32), 0)
        nc.vector.memset(v_plane1[:].bitcast(I32), 0)
        identity = tile([P, P], F32, "identity")
        make_identity(nc, identity[:])
        one = tile([P, 1], F32, "one")
        half_pi = tile([P, 1], F32, "half_pi")
        nc.vector.memset(one[:], 1.0)
        nc.scalar.activation(half_pi[:], one[:], ACT.Copy, scale=math.pi / 2)

        def load_plane(plane, scales, passes):
            for q in range(QUADS):
                nc.gpsimd.dma_start(
                    plane[QUAD * q : QUAD * q + 4 * passes, :].bitcast(I32),
                    scales[:, 4 * q : 4 * q + 4, :].bitcast(I32),
                )

        def load_weight(w, a, b):
            raw = tile([P, PACK, BANK], F32, "raw", bufs=3)
            rows = w[PASS * a : PASS * (a + 1), BANK * b : BANK * (b + 1)]
            nc.sync.dma_start(raw[:], rows.rearrange("(p j) c -> p j c", j=PACK))
            return raw

        def quantise_weight(raw, name, copy):
            rounded = tile([P, BANK * PACK], BF16, "rounded", bufs=3)
            copy(
                rounded[:].rearrange("p (u e m j) -> p u m j e", u=2, e=2, j=PACK),
                raw[:].rearrange("p j (m u e) -> p u m j e", u=2, e=2),
            )
            codes = tile([P, BANK], U32, name + "_codes")
            plane = tile([P, BANK], U8, name + "_plane")
            nc.vector.quantize_mx(out=codes[:].bitcast(E4M3), scales=plane[:], in_=rounded[:])
            return codes, plane

        def load_table(words, a, width, tag):
            window = tile([P, width], I32, tag)
            nc.sync.dma_start(window[:], words[a].rearrange("p t i -> p (t i)").bitcast(I32))
            return window

        def gather(window, offsets, count, dtype, name):
            picked = tile([P, count], dtype, name)
            nc.vector.tensor_copy(picked[:], window[:].bitcast(dtype).indirect(offsets[:]))
            return picked

        w2_raw = {(a, 0): load_weight(w2, a, 0) for a in range(m_passes)}
        load_plane(tab2_plane, tab2_scales, m_passes)
        tab2_win = [load_table(tab2_words, a, TG, "tab2_%d" % a) for a in range(m_passes)]
        load_plane(tab_plane, tab_scales, k_passes)
        for q in range(QUADS):
            nc.scalar.dma_start(
                w1_plane_raw[QUAD * q : QUAD * q + 4, :, :].bitcast(I32),
                w1_scales[:, 4 * q : 4 * q + 4, :].rearrange("a r c -> r a c").bitcast(I32),
            )
        b1_col = tile([P, r_passes, PACK], F32, "b1_col")
        gz_col = tile([P, r_passes, PACK], F32, "gz_col")
        pages = {}

        def open_page(b, t, tag=None):
            pages[b, t] = tile([P, S], F32, "page%d%d" % (b, t), tag=tag)
            nc.gpsimd.memset(pages[b, t][:], 0.0)

        early = [(b, t) for b in range(r_passes) for t in range(PACK)][:-k_passes]
        late = [(r_passes - 1, PACK - k_passes + a) for a in range(k_passes)]
        for b, t in early:
            open_page(b, t)

        turned = bank([P, G // P, P], "wide")
        for jb in range(G // P):
            nc.tensor.transpose(turned[:, jb, :], wgs_raw[:, P * jb : P * (jb + 1)], identity[:])
        wgs_cols = tile([P, G // P, PACK, QUADS, QUAD], F32, "wgs_cols", tag="cosine0")
        for q in range(QUADS):
            nc.scalar.copy(wgs_cols[:, :, :, q, :], turned[:].rearrange("p b (m t) -> p b t m", t=PACK))
        wgs_rows = tile([P, PACK, G], F32, "wgs_rows")
        for t in range(PACK):
            back = bank([P, G // P, P], "wide")
            for jb in range(G // P):
                nc.tensor.transpose(
                    back[:, jb, :], wgs_cols[:, jb, t, :, :].rearrange("p q m -> p (q m)"), identity[:]
                )
            nc.scalar.copy(wgs_rows[:, t, :], back[:].rearrange("p b j -> p (b j)"))

        w2_q = {}
        for a in range(m_passes):
            w2_q[a, 0] = quantise_weight(w2_raw[a, 0], "w2_%d_0" % a, nc.vector.tensor_copy if a == m_passes - 1 else nc.scalar.copy)
        v2_plane = gather(tab2_plane, idx2, G, U8, "v2_plane")
        v2_words = [gather(tab2_win[a], idx2, G, U32, "v2_words%d" % a) for a in range(m_passes)]
        v_plane0 = gather(tab_plane, idx, S, U8, "v_plane0")
        w1_plane = tile([P, k_passes, H], U8, "w1_plane")
        nc.vector.tensor_copy(
            w1_plane[:].rearrange("p a (b t m) -> p (a b) t m", t=PACK, m=P),
            w1_plane_raw[:].rearrange("p a (b m t) -> p (a b) t m", t=PACK, m=P),
        )

        for a in range(m_passes):
            w2_raw[a, 1] = load_weight(w2, a, 1)
        tab_win = [load_table(tab_words, a, T, "tab_%d" % a) for a in range(k_passes)]
        nc.sync.dma_start(gz_col[:], gz.rearrange("(b p t) -> p b t", p=P, t=PACK))
        nc.sync.dma_start(b1_col[:], b1.rearrange("(b p t) -> p b t", p=P, t=PACK))
        moved = QUAD * (QUADS - 1) + 4
        nc.gpsimd.dma_start(v_plane1[0:moved, :].bitcast(I32), v_plane0[4 : 4 + moved, :].bitcast(I32))
        v_planes = [v_plane0, v_plane1]
        w1_raw = tile([P, k_passes, 2 * H], U8, "w1_raw")
        nc.sync.dma_start(w1_raw[:].bitcast(I32), w1_words.rearrange("a p c -> p a c").bitcast(I32))
        w3_raw = [load_weight(w3, b, 0) for b in range(r_passes)]

        def place(b, t):
            acc = bank([P, BANK], "acc")
            cols = slice(P * t, P * (t + 1))
            for a in range(m_passes):
                codes, plane = w2_q[a, b]
                nc.tensor.matmul_mx(
                    out=acc[:], lhsT=codes[:, cols].bitcast(E4M3), lhsT_scale=plane[:, cols],
                    rhs=v2_words[a][:].bitcast(E4M3), rhs_scale=v2_plane[4 * a : P, :],
                    start=(a == 0), stop=(a == m_passes - 1),
                )
            offsets = tile([P, G], F32, "offsets", bufs=4)
            nc.scalar.copy(offsets[:], acc[:])
            nc.vector.tensor_tensor(pages[b, t][:].indirect(slot[:]), offsets[:], wgs_rows[:, t, :], ALU.mult)

        def take_cosine(b, t):
            size = tile([P, S], F32, "size", bufs=2)
            nc.scalar.activation(size[:], pages[b, t][:], ACT.Abs)
            nc.scalar.activation(cosines[b, t], size[:], ACT.Sin, bias=half_pi[:], scale=-1.0)

        for t in range(PACK):
            place(0, t)
        for a in range(m_passes):
            w2_q[a, 1] = quantise_weight(w2_raw[a, 1], "w2_%d_1" % a, nc.scalar.copy)
        cosine0 = tile([P, PACK, S], F32, "cosine0")
        cosines = {(0, t): cosine0[:, t, :] for t in range(PACK)}
        for b, t in early[PACK:]:
            place(b, t)
        for t in range(PACK):
            take_cosine(0, t)

        v_words = [gather(tab_win[a], idx, S, U32, "v_words%d" % a) for a in range(k_passes)]
        for a, (b, t) in enumerate(late):
            open_page(b, t, tag="tab_%d" % a)
            place(b, t)
        w1_codes = tile([P, k_passes, 2 * H], U8, "w1_codes")
        nc.scalar.copy(
            w1_codes[:].bitcast(U16).rearrange("p a (b t m) -> p (a b) t m", t=PACK, m=P),
            w1_raw[:].bitcast(U16).rearrange("p a (b m t) -> p (a b) t m", t=PACK, m=P),
        )
        w3_q = [quantise_weight(w3_raw[b], "w2_%d_0" % b, nc.scalar.copy) for b in range(r_passes)]
        for pair, tag in enumerate(("tab2_2", "cosine1")):
            cosine1 = tile([P, 2, S], F32, "cosine1_%d" % pair, tag=tag)
            for e in range(2):
                cosines[1, 2 * pair + e] = cosine1[:, e, :]
        for t in range(PACK):
            take_cosine(1, t)

        z_rows = [tile([P, PACK, S], BF16, "z_rows%d" % b, tag="tab2_%d" % b) for b in range(r_passes)]

        def modulate(b, t, js):
            acc = bank([P, js.stop - js.start], "acc")
            first = BANK * b + P * t
            for a in range(k_passes):
                nc.tensor.matmul_mx(
                    out=acc[:],
                    lhsT=w1_codes[:, a, 2 * first : 2 * (first + P)].bitcast(E2M1),
                    lhsT_scale=w1_plane[:, a, first : first + P],
                    rhs=v_words[a][:, js].bitcast(E4M3), rhs_scale=v_planes[a][:, js],
                    start=(a == 0), stop=(a == k_passes - 1),
                )
            cosine = cosines[b, t][:, js]
            nc.vector.scalar_tensor_tensor(cosine, acc[:], b1_col[:, b, t : t + 1], cosine, ALU.add, ALU.mult)

        def join(b, t, js):
            nc.vector.scalar_tensor_tensor(
                z_rows[b][:, t, js], pages[b, t][:, js], gz_col[:, b, t : t + 1], cosines[b, t][:, js],
                ALU.mult, ALU.add,
            )

        z_codes = [tile([P, S], U32, "z_codes%d" % b) for b in range(r_passes)]
        z_plane = [tile([P, S], U8, "z_plane%d" % b) for b in range(r_passes)]

        def make_z(b, js, copy):
            for t in range(PACK + 1):
                if t < PACK:
                    modulate(b, t, js)
                if t > 0:
                    join(b, t - 1, js)
            woven = tile([P, (js.stop - js.start) * PACK], BF16, "rounded", bufs=3)
            copy(
                woven[:].rearrange("p (c i t) -> p c t i", i=RUN, t=PACK),
                z_rows[b][:, :, js].rearrange("p t (c i) -> p c t i", i=RUN),
            )
            nc.vector.quantize_mx(out=z_codes[b][:, js].bitcast(E4M3), scales=z_plane[b][:, js], in_=woven[:])

        y_codes = tile([P, S], U32, "y_codes")
        y_plane = tile([P, S], U8, "y_plane")
        out_rows = out_0.rearrange("(p t) j -> p t j", t=PACK)
        out_words = out_1[0].rearrange("p m t -> p (m t)").bitcast(I32)

        def project(u):
            y = tile([P, PACK, QUARTER], F32, "y", tag="raw", bufs=3)
            rounded = tile([P, QUARTER * PACK], BF16, "y_rounded", bufs=2)
            for c in range(QUARTER // P):
                acc = bank([P, PACK, P], "wide")
                first = QUARTER * u + P * c
                js = slice(first, first + P)
                for b in range(r_passes):
                    for t in range(PACK):
                        cols = slice(P * t, P * (t + 1))
                        nc.tensor.matmul_mx(
                            out=acc[:, t, :], lhsT=w3_q[b][0][:, cols].bitcast(E4M3), lhsT_scale=w3_q[b][1][:, cols],
                            rhs=z_codes[b][:, js].bitcast(E4M3), rhs_scale=z_plane[b][:, js],
                            start=(b == 0 and t == 0), stop=(b == r_passes - 1 and t == PACK - 1),
                        )
                nc.scalar.copy(y[:, :, P * c : P * (c + 1)], acc[:])
                woven = rounded[:, PACK * P * c : PACK * P * (c + 1)].rearrange("p (j t) -> p j t", t=PACK)
                if u < S // QUARTER - 1:
                    nc.scalar.copy(woven, acc[:].rearrange("p t j -> p j t"))
                else:
                    nc.vector.tensor_copy(woven, acc[:].rearrange("p t j -> p j t"))
            js = slice(QUARTER * u, QUARTER * (u + 1))
            nc.sync.dma_start(out_rows[:, :, js], y[:])
            nc.vector.quantize_mx(out=y_codes[:, js].bitcast(E4M3), scales=y_plane[:, js], in_=rounded[:])
            nc.sync.dma_start(out_words[:, js], y_codes[:, js].bitcast(I32))

        make_z(0, slice(0, BANK), nc.scalar.copy)
        make_z(1, slice(0, BANK), nc.scalar.copy)
        make_z(0, slice(BANK, S), nc.scalar.copy)
        project(0)
        project(1)
        make_z(1, slice(BANK, BANK + QUARTER), nc.vector.tensor_copy)
        make_z(1, slice(BANK + QUARTER, S), nc.vector.tensor_copy)
        project(2)
        project(3)
        for q in range(QUADS):
            queue = nc.scalar if q % 2 else nc.sync
            queue.dma_start(out_2[0, 4 * q : 4 * q + 4, :].bitcast(I32), y_plane[QUAD * q : QUAD * q + 4, :].bitcast(I32))
